import numpy as np
CORES = [7,135,263,391,15,143,271,399,23,151,279,407,31,159,287,415]
N = 16
GROUPS = [[0,1,4,5,8,9,12,13],[2,3,6,7,10,11,14,15]]
def setup_inputs(rng):
    return {"x": rng.standard_normal((N, 128, 128), dtype=np.float32)}
def reference(x):
    y = np.empty((N, 128, 1024), x.dtype)
    for g in GROUPS:
        s = np.concatenate([x[r] for r in g], axis=1)
        for r in g:
            y[r] = s
    return {"y": y}

@@ -1,0 +1,31 @@
+from concourse.bass import DstId, RemoteDMATransfer
+
+SCRATCH = {
+    "land": ("sbuf", [128, 1024], "float32"),
+}
+SEMAPHORES = ["loaded", "arrived", "stored"]
+
+
+def rank_program(g, core, T, topo):
+    rank = T.rank_of(core)
+    if rank is None:
+        return
+    group = [grp for grp in T.tables["GROUPS"] if rank in grp][0]
+    w = T.x.shape[1]
+    j = group.index(rank)
+    mine = T.land[:, j * w:(j + 1) * w]
+    g.sync.dma_start(mine, T.x[:]).then_inc(T.sem.loaded, 16)
+    g.wait_ge(T.sem.loaded, 16)
+    peers = [T.cores[r] for r in group if r != rank]
+    ids = []
+    for d in peers:
+        rid, pid = topo.addr(d, core)
+        ids.append(DstId(rid=rid, pnc=pid))
+    g.remote_dma_fused(
+        [RemoteDMATransfer(dst_ids=ids, dma_engine_mask=0xFF, remote_sem=T.sem.arrived,
+                           srcs=[mine], dsts=[mine for d in peers])],
+        local_sem=T.sem.arrived)
+    g.wait_ge(T.sem.arrived, 8 * len(group))
+    g.sync.wait_ge(T.sem.arrived, 8 * len(group))
+    g.sync.dma_start(T.y[:], T.land[:]).then_inc(T.sem.stored, 16)
+    g.wait_ge(T.sem.stored, 16)

@@ -1,31 +1,85 @@
 from concourse.bass import DstId, RemoteDMATransfer
 
+HELPER = 3
+OFF_CHIP = 0x00FF
+ON_CHIP = 0xFF00
+
 SCRATCH = {
-    "land": ("sbuf", [128, 1024], "float32"),
+    "land": ("dram", [8, 128, 128], "float32"),
 }
-SEMAPHORES = ["loaded", "arrived", "stored"]
+SEMAPHORES = ["a%d" % k for k in range(8)] + ["loaded", "sent", "stored"]
+
+
+def dst_id(topo, dst, src):
+    rid, pid = topo.addr(dst, src)
+    return DstId(rid=rid, pnc=pid)
+
+
+def members_of(T, rank):
+    group = [grp for grp in T.tables["GROUPS"] if rank in grp][0]
+    return [T.cores[r] for r in group]
 
 
 def rank_program(g, core, T, topo):
     rank = T.rank_of(core)
     if rank is None:
+        owner = core - core % 8 + 7
+        if core % 8 == HELPER and T.rank_of(owner) is not None:
+            helper_program(g, core, owner, T, topo)
         return
-    group = [grp for grp in T.tables["GROUPS"] if rank in grp][0]
+
+    cores = members_of(T, rank)
+    me = cores.index(core)
     w = T.x.shape[1]
-    j = group.index(rank)
-    mine = T.land[:, j * w:(j + 1) * w]
-    g.sync.dma_start(mine, T.x[:]).then_inc(T.sem.loaded, 16)
+    arrived = [T.sem["a%d" % k] for k in range(len(cores))]
+    helper = core - core % 8 + HELPER
+
+    far = [k for k, c in enumerate(cores) if topo.host(c) != topo.host(core)]
+    plane = sorted([k for k in far if topo.same_plane(cores[k], core)],
+                   key=lambda k: topo.chip(cores[k]) != topo.chip(core))
+    relayed = [k for k in far if k not in plane]
+    relayed.sort(key=lambda k: topo.chip(cores[k]) ^ 1 != topo.chip(core))
+    near = [k for k, c in enumerate(cores) if topo.host(c) == topo.host(core) and k != me]
+    mate = [c for c in cores if topo.mates(c, core)][0]
+
+    def store(q, k, src):
+        q.dma_start(T.y[:, k * w:(k + 1) * w], src).then_inc(T.sem.stored, 16)
+
+    g.sync.dma_start(T.land[me], T.x[:]).then_inc(T.sem.loaded, 16)
+    store(g.scalar, me, T.x[:])
+
     g.wait_ge(T.sem.loaded, 16)
-    peers = [T.cores[r] for r in group if r != rank]
-    ids = []
-    for d in peers:
-        rid, pid = topo.addr(d, core)
-        ids.append(DstId(rid=rid, pnc=pid))
     g.remote_dma_fused(
-        [RemoteDMATransfer(dst_ids=ids, dma_engine_mask=0xFF, remote_sem=T.sem.arrived,
-                           srcs=[mine], dsts=[mine for d in peers])],
-        local_sem=T.sem.arrived)
-    g.wait_ge(T.sem.arrived, 8 * len(group))
-    g.sync.wait_ge(T.sem.arrived, 8 * len(group))
-    g.sync.dma_start(T.y[:], T.land[:]).then_inc(T.sem.stored, 16)
-    g.wait_ge(T.sem.stored, 16)
+        [RemoteDMATransfer(dst_ids=[dst_id(topo, helper, core)], dma_engine_mask=ON_CHIP, remote_sem=arrived[me],
+                           srcs=[T.land[me]], dsts=[T.land[me]]),
+         RemoteDMATransfer(dst_ids=[dst_id(topo, cores[k], core) for k in plane], dma_engine_mask=OFF_CHIP,
+                           remote_sem=arrived[me], srcs=[T.land[me]], dsts=[T.land[me] for k in plane])],
+        local_sem=T.sem.sent)
+
+    rid, pid = topo.addr(mate, core)
+    for k in plane:
+        g.wait_ge(arrived[k], 8)
+        g.remote_dma(T.land[k], T.land[k], arrived[k], T.sem.sent, pid, rid, OFF_CHIP)
+
+    due = plane + near + relayed
+    for i, k in enumerate(due):
+        q = g.sync if i % 2 == 0 else g.scalar
+        q.wait_ge(arrived[k], 8)
+        store(q, k, T.land[k])
+
+    g.wait_ge(T.sem.sent, 16 + 8 * len(plane))
+    for k in near + relayed:
+        g.wait_ge(arrived[k], 8)
+    g.wait_ge(T.sem.stored, 16 * len(cores))
+
+
+def helper_program(g, core, owner, T, topo):
+    cores = members_of(T, T.rank_of(owner))
+    k = cores.index(owner)
+    near = [c for c in cores if topo.host(c) == topo.host(owner) and c != owner]
+    g.wait_ge(T.sem["a%d" % k], 8)
+    g.remote_dma_fused(
+        [RemoteDMATransfer(dst_ids=[dst_id(topo, c, core) for c in near], dma_engine_mask=OFF_CHIP,
+                           remote_sem=T.sem["a%d" % k], srcs=[T.land[k]], dsts=[T.land[k] for c in near])],
+        local_sem=T.sem.sent)
+    g.wait_ge(T.sem.sent, 8)

from concourse.bass import DstId, RemoteDMATransfer

HELPER = 3
OFF_CHIP = 0x00FF
ON_CHIP = 0xFF00

SCRATCH = {
    "land": ("dram", [8, 128, 128], "float32"),
}
SEMAPHORES = ["a%d" % k for k in range(8)] + ["loaded", "sent", "stored"]


def dst_id(topo, dst, src):
    rid, pid = topo.addr(dst, src)
    return DstId(rid=rid, pnc=pid)


def members_of(T, rank):
    group = [grp for grp in T.tables["GROUPS"] if rank in grp][0]
    return [T.cores[r] for r in group]


def rank_program(g, core, T, topo):
    rank = T.rank_of(core)
    if rank is None:
        owner = core - core % 8 + 7
        if core % 8 == HELPER and T.rank_of(owner) is not None:
            helper_program(g, core, owner, T, topo)
        return

    cores = members_of(T, rank)
    me = cores.index(core)
    w = T.x.shape[1]
    arrived = [T.sem["a%d" % k] for k in range(len(cores))]
    helper = core - core % 8 + HELPER

    far = [k for k, c in enumerate(cores) if topo.host(c) != topo.host(core)]
    plane = sorted([k for k in far if topo.same_plane(cores[k], core)],
                   key=lambda k: topo.chip(cores[k]) != topo.chip(core))
    relayed = [k for k in far if k not in plane]
    relayed.sort(key=lambda k: topo.chip(cores[k]) ^ 1 != topo.chip(core))
    near = [k for k, c in enumerate(cores) if topo.host(c) == topo.host(core) and k != me]
    mate = [c for c in cores if topo.mates(c, core)][0]

    def store(q, k, src):
        q.dma_start(T.y[:, k * w:(k + 1) * w], src).then_inc(T.sem.stored, 16)

    g.sync.dma_start(T.land[me], T.x[:]).then_inc(T.sem.loaded, 16)
    store(g.scalar, me, T.x[:])

    g.wait_ge(T.sem.loaded, 16)
    g.remote_dma_fused(
        [RemoteDMATransfer(dst_ids=[dst_id(topo, helper, core)], dma_engine_mask=ON_CHIP, remote_sem=arrived[me],
                           srcs=[T.land[me]], dsts=[T.land[me]]),
         RemoteDMATransfer(dst_ids=[dst_id(topo, cores[k], core) for k in plane], dma_engine_mask=OFF_CHIP,
                           remote_sem=arrived[me], srcs=[T.land[me]], dsts=[T.land[me] for k in plane])],
        local_sem=T.sem.sent)

    rid, pid = topo.addr(mate, core)
    for k in plane:
        g.wait_ge(arrived[k], 8)
        g.remote_dma(T.land[k], T.land[k], arrived[k], T.sem.sent, pid, rid, OFF_CHIP)

    due = plane + near + relayed
    for i, k in enumerate(due):
        q = g.sync if i % 2 == 0 else g.scalar
        q.wait_ge(arrived[k], 8)
        store(q, k, T.land[k])

    g.wait_ge(T.sem.sent, 16 + 8 * len(plane))
    for k in near + relayed:
        g.wait_ge(arrived[k], 8)
    g.wait_ge(T.sem.stored, 16 * len(cores))


def helper_program(g, core, owner, T, topo):
    cores = members_of(T, T.rank_of(owner))
    k = cores.index(owner)
    near = [c for c in cores if topo.host(c) == topo.host(owner) and c != owner]
    g.wait_ge(T.sem["a%d" % k], 8)
    g.remote_dma_fused(
        [RemoteDMATransfer(dst_ids=[dst_id(topo, c, core) for c in near], dma_engine_mask=OFF_CHIP,
                           remote_sem=T.sem["a%d" % k], srcs=[T.land[k]], dsts=[T.land[k] for c in near])],
        local_sem=T.sem.sent)
    g.wait_ge(T.sem.sent, 8)
